import numpy as np
import ml_dtypes


def mxq(x, axis, fmt="e4m3"):
    dtype, down = {"e4m3": (ml_dtypes.float8_e4m3fn, 7), "e5m2": (ml_dtypes.float8_e5m2, 14)}[fmt]
    v = np.moveaxis(np.asarray(x, np.float32).astype(ml_dtypes.bfloat16).astype(np.float64), axis, -1)
    blocks = v.reshape(v.shape[:-1] + (-1, 32))
    amax = np.abs(blocks).max(-1, keepdims=True)
    byte = np.maximum(np.where(amax > 0, np.frexp(amax)[1] - 1 + 127, 0) - down, 1)
    scale = np.exp2(byte - 127.0)
    codes = (blocks / scale).astype(np.float32).astype(dtype).astype(np.float64)
    return np.moveaxis((codes * scale).reshape(v.shape), -1, axis)


WIDE = False


def mx_kscale(k):
    if not WIDE:
        return np.ones(k)
    levels = np.array([10, -10, 5, -5, 0])
    if k % 512:
        return np.exp2(np.random.permutation(np.resize(levels, k // 32))).repeat(32)
    a = np.empty((k // 512, 16))
    for p in range(k // 512):
        a[p, :8] = np.random.permutation(np.resize(levels, 8))
        for g in range(8):
            far = levels[np.abs(levels - a[p, g]) >= 10]
            a[p, g + 8] = far[np.random.randint(len(far))]
    return np.exp2(a.ravel()).repeat(32)


def f64(x):
    return np.asarray(x).astype(np.float64)


def striped(idx):
    return np.tile(np.asarray(idx).reshape(-1, 16).T, (8, 1)).astype(np.uint16)


def unstriped(offs):
    return offs[:16].T.reshape(-1).astype(np.int64)


E2M1 = np.array([0.0, 0.5, 1.0, 1.5, 2.0, 3.0, 4.0, 6.0, -0.0, -0.5, -1.0, -1.5, -2.0, -3.0, -4.0, -6.0])


def pack_weight(w, fmt):
    k, n = w.shape
    w = f64(np.asarray(w, np.float32).astype(ml_dtypes.bfloat16)).reshape(k // 32, 32, n)
    amax = np.abs(w).max(1)
    if fmt == "e4m3":
        byte = np.frexp(amax)[1] - 1 + 127 - 7
    else:
        mant, ex = np.frexp(amax / 6.0)
        byte = np.where(mant > 0.5, ex, ex - 1) + 127
    byte = np.clip(np.where(amax > 0, byte, 1), 1, 254)
    scaled = (w * np.exp2(127.0 - byte)[:, None, :]).reshape(k, n).astype(np.float32)
    by_word = np.ascontiguousarray(scaled.reshape(k // 512, 128, 4, n).transpose(0, 1, 3, 2))
    if fmt == "e4m3":
        words = by_word.astype(ml_dtypes.float8_e4m3fn).view(np.uint8)
    else:
        c = by_word.astype(ml_dtypes.float4_e2m1fn).view(np.uint8) & 0xF
        words = (c[..., 0::2] | (c[..., 1::2] << 4)).reshape(k // 512, 128, 2 * n)
    return np.ascontiguousarray(words), np.ascontiguousarray(byte.astype(np.uint8).reshape(k // 512, 16, n))


def unpack_weight(words, scales, fmt):
    g, _, n = scales.shape
    words = np.ascontiguousarray(words).reshape(g, 128, n, -1)
    if fmt == "e4m3":
        vals = words.view(ml_dtypes.float8_e4m3fn).astype(np.float64)
    else:
        nib = np.empty((g, 128, n, 4), np.uint8)
        nib[..., 0::2] = words & 0xF
        nib[..., 1::2] = words >> 4
        vals = E2M1[nib]
    vals = vals * np.repeat(np.exp2(scales.astype(np.float64) - 127.0), 8, axis=1)[..., None]
    return vals.transpose(0, 1, 3, 2).reshape(g * 512, n)


def sigmoid(v):
    return 1.0 / (1.0 + np.exp(-v))


def bf(x):
    return np.asarray(x, np.float32).astype(ml_dtypes.bfloat16)


def planes(Y):
    r, m = Y.shape
    b = f64(bf(Y)).reshape(r // 32, 32, m)
    amax = np.abs(b).max(1)
    byte = np.clip(np.where(amax > 0, np.frexp(amax)[1] - 1 + 127 - 7, 1), 1, 254)
    codes = (b * np.exp2(127.0 - byte)[:, None, :]).reshape(r, m).astype(np.float32).astype(ml_dtypes.float8_e4m3fn).view(np.uint8)
    words = codes.reshape(r // 512, 128, 4, m).transpose(0, 1, 3, 2)
    return np.ascontiguousarray(words), np.ascontiguousarray(byte.astype(np.uint8).reshape(r // 512, 16, m))


K, L, T, J, N = 1024, 512, 2048, 512, 512


def setup_inputs():
    n = np.random.standard_normal
    idx = np.random.permutation(T)[:J]
    fk = mx_kscale(K)
    fl = mx_kscale(L)
    wvp = pack_weight(n((K, N)) * 1 / np.sqrt(K) * fk[:, None], "e2m1")
    gxp = pack_weight(n((L, J)) / fl[:, None], "e4m3")
    wgp = pack_weight(n((L, N)) * 1 / np.sqrt(L) * fl[:, None], "e2m1")
    return {
        "xt": (n((K, J)) / fk[:, None]).astype(np.float32),
        "wv_words": wvp[0],
        "wv_scales": wvp[1],
        "gx_words": gxp[0],
        "gx_scales": gxp[1],
        "wg_words": wgp[0],
        "wg_scales": wgp[1],
        "old": (1.0 * n((N, T))).astype(np.float32),
        "offs": striped(idx),
    }


def reference(xt, wv_words, wv_scales, gx_words, gx_scales, wg_words, wg_scales, old, offs):
    idx = unstriped(offs)
    wvu = unpack_weight(wv_words, wv_scales, "e2m1")
    gxu = unpack_weight(gx_words, gx_scales, "e4m3")
    wgu = unpack_weight(wg_words, wg_scales, "e2m1")
    xtq = mxq(f64(xt), 0, "e4m3")
    v = wvu.T @ xtq
    g = wgu.T @ gxu
    d = sigmoid(g) * (v - f64(old)[:, idx])
    p = np.zeros((N, T))
    p[:, idx] = d
    y = f64(old) + p
    words, scales = planes(y)
    return y, words, scales

@@ -1,0 +1,255 @@
+from contextlib import ExitStack
+
+import concourse.mybir as mybir
+
+K, L, T, J, N = 1024, 512, 2048, 512, 512
+FLOPS = 2 * (K + L) * N * J
+
+F32 = mybir.dt.float32
+BF16 = mybir.dt.bfloat16
+I32 = mybir.dt.int32
+U32 = mybir.dt.uint32
+U16 = mybir.dt.uint16
+U8 = mybir.dt.uint8
+FP8X4 = mybir.dt.float8_e4m3fn_x4
+FP4X4 = mybir.dt.float4_e2m1fn_x4
+ACT = mybir.ActivationFunctionType
+ALU = mybir.AluOpType
+
+P = 128
+PACK = 4
+PASSES = K // (P * PACK)
+HALVES = 2
+JH = J // HALVES
+CHUNKS = 4
+TC = T // CHUNKS
+PAGES = 3
+VECTOR_SCATTERS = ((0, 0), (1, 1))
+ROUNDS = ((0, 0, TC, False), (1, 0, TC, False), (2, 0, TC // 2, False), (2, TC // 2, TC, True), (3, 0, TC, True))
+
+
+def tile_list_page_drift_pl_kernel(
+    tc, xt, wv_words, wv_scales, gx_words, gx_scales, wg_words, wg_scales, old, offs, out_0, out_1, out_2
+):
+    nc = tc.nc
+    with ExitStack() as ctx:
+        keep = ctx.enter_context(tc.tile_pool(name="keep", bufs=1))
+        psum = ctx.enter_context(tc.psum_pool(name="psum", bufs=1))
+
+        def sb(name, shape, dtype):
+            return keep.tile(shape, dtype, name=name, align_bytes=64)
+
+        offsets = keep.tile([P, J // 16], U16, name="offsets")
+        x_raw = {(z, h): sb(f"x_raw{z}{h}", [P, PACK, JH], F32) for z in range(PASSES) for h in range(HALVES)}
+        x_bf = {(z, h): sb(f"x_bf{z}{h}", [P, JH * PACK], BF16) for z in range(PASSES) for h in range(HALVES)}
+        x_codes = [sb(f"x_codes{z}", [P, J], U32) for z in range(PASSES)]
+        x_scales = [sb(f"x_scales{z}", [P, J], U8) for z in range(PASSES)]
+        wv_raw = sb("wv_raw", [P, PASSES, 2 * N], U8)
+        wv_dealt = sb("wv_dealt", [P, PASSES, 2 * N], U8)
+        wvs_raw = sb("wvs_raw", [P, PASSES, N], U8)
+        wvs_dealt = sb("wvs_dealt", [P, PASSES, N], U8)
+        wg_raw = sb("wg_raw", [P, 1, 2 * N], U8)
+        wg_dealt = sb("wg_dealt", [P, 1, 2 * N], U8)
+        wgs_raw = sb("wgs_raw", [P, 1, N], U8)
+        wgs_dealt = sb("wgs_dealt", [P, 1, N], U8)
+        gx_codes = sb("gx_codes", [P, J], U32)
+        gx_plane = sb("gx_plane", [P, 1, J], U8)
+        old_rows = [sb(f"old_rows{t}", [P, T], F32) for t in range(PACK)]
+        pages = [sb(f"page{i}", [P, T], F32) for i in range(PAGES)]
+        gate = [sb(f"gate{t}", [P, J], F32) for t in range(PACK)]
+        y = sb("y", [P, CHUNKS, PACK, TC], F32)
+        y_plane = sb("y_plane", [P, T], U8)
+        g_bank = [psum.tile([P, J], F32, name=f"g_bank{t}") for t in range(PACK)]
+        v_bank = [psum.tile([P, JH], F32, name=f"v_bank{t}") for t in range(PACK)]
+
+        def v_of(t, h):
+            return v_bank[t][:] if h == 0 else g_bank[t][:, 0:JH]
+
+        old_by_t = old.rearrange("(p t) c -> p t c", t=PACK)
+        out_by_t = out_0.rearrange("(p t) c -> p t c", t=PACK)
+
+        def half(h):
+            return slice(h * JH, (h + 1) * JH)
+
+        def load_x(z, h):
+            rows = xt[z * P * PACK : (z + 1) * P * PACK, h * JH : (h + 1) * JH]
+            nc.sync.dma_start(out=x_raw[z, h][:], in_=rows.rearrange("(p i) j -> p i j", i=PACK))
+
+        def load_words(tile, words):
+            nc.sync.dma_start(out=tile[:].bitcast(I32), in_=words.rearrange("z p b -> p z b").bitcast(I32))
+
+        def load_plane(queue, tile, scales):
+            for q in range(4):
+                queue.dma_start(
+                    out=tile[32 * q : 32 * q + 4].bitcast(I32),
+                    in_=scales[:, 4 * q : 4 * q + 4, :].rearrange("z r n -> r z n").bitcast(I32),
+                )
+
+        def load_plane_repeated(tile, scales):
+            for q in range(4):
+                rows = scales[0, 4 * q : 4 * q + 4, :].bitcast(I32)
+                nc.sync.dma_start(
+                    out=tile[32 * q : 32 * q + 32, 0, :].bitcast(I32),
+                    in_=rows.unsqueeze(0).to_broadcast([8, 4, rows.shape[1]]),
+                )
+
+        def load_old(t):
+            nc.sync.dma_start(out=old_rows[t][:], in_=old_by_t[:, t, :])
+
+        def deal(dealt, raw, run, ts):
+            nc.vector.tensor_copy(
+                out=dealt.rearrange("p z (t c i) -> p z c t i", t=PACK, i=run)[:, :, :, ts, :],
+                in_=raw.rearrange("p z (c i t) -> p z c t i", t=PACK, i=run)[:, :, :, ts, :],
+            )
+
+        def round_and_interleave(copy, dst, src):
+            copy(
+                out=dst.rearrange("p (c i t) -> p c t i", i=4, t=PACK),
+                in_=src.rearrange("p t (c i) -> p c t i", i=4),
+            )
+
+        def quantise_x(z, h):
+            copy = nc.scalar.copy if (z, h) == (0, 1) else nc.vector.tensor_copy
+            round_and_interleave(copy, x_bf[z, h][:], x_raw[z, h][:])
+            nc.vector.quantize_mx(
+                out=x_codes[z][:, half(h)].bitcast(FP8X4), scales=x_scales[z][:, half(h)], in_=x_bf[z, h][:]
+            )
+
+        def new_values(t, h):
+            cols = half(h)
+            for z in range(PASSES):
+                nc.tensor.matmul_mx(
+                    out=v_of(t, h),
+                    lhsT=wv_dealt[:, z, 2 * P * t : 2 * P * (t + 1)].bitcast(FP4X4),
+                    lhsT_scale=wvs_dealt[:, z, P * t : P * (t + 1)],
+                    rhs=x_codes[z][:, cols].bitcast(FP8X4),
+                    rhs_scale=x_scales[z][:, cols],
+                    start=(z == 0),
+                    stop=(z == PASSES - 1),
+                )
+
+        def gates(t):
+            nc.tensor.matmul_mx(
+                out=g_bank[t][:],
+                lhsT=wg_dealt[:, 0, 2 * P * t : 2 * P * (t + 1)].bitcast(FP4X4),
+                lhsT_scale=wgs_dealt[:, 0, P * t : P * (t + 1)],
+                rhs=gx_codes[:].bitcast(FP8X4),
+                rhs_scale=gx_plane[:, 0, :],
+                start=True,
+                stop=True,
+            )
+            nc.scalar.activation(out=gate[t][:], in_=g_bank[t][:], func=ACT.Sigmoid)
+
+        def listed(h):
+            return offsets[:, h * (JH // 16) : (h + 1) * (JH // 16)]
+
+        picked = {(t, h): sb(f"picked{t}{h}", [P, JH], F32)[:] for t in range(PACK) for h in range(HALVES)}
+        gap = {th: sb(f"gap{th[0]}{th[1]}", [P, JH], F32)[:] for th in picked}
+        steps = {th: sb(f"step{th[0]}{th[1]}", [P, JH], F32)[:] for th in picked if th not in VECTOR_SCATTERS}
+
+        def pick(t, h):
+            nc.scalar.activation(out=picked[t, h], in_=old_rows[t][:].indirect(listed(h)), func=ACT.Copy)
+
+        def distance(t, h):
+            nc.vector.tensor_tensor(out=gap[t, h], in0=v_of(t, h), in1=picked[t, h], op=ALU.subtract)
+
+        def step(t, h):
+            nc.vector.tensor_tensor(out=steps[t, h], in0=gap[t, h], in1=gate[t][:, half(h)], op=ALU.mult)
+
+        def put(t, h):
+            places = pages[t % PAGES][:].indirect(listed(h))
+            if (t, h) in VECTOR_SCATTERS:
+                nc.vector.tensor_tensor(out=places, in0=gap[t, h], in1=gate[t][:, half(h)], op=ALU.mult)
+            else:
+                nc.scalar.activation(out=places, in_=steps[t, h], func=ACT.Copy)
+
+        def drift(t, chunks):
+            cols = slice(chunks.start * TC, chunks.stop * TC)
+            nc.vector.tensor_tensor(
+                out=y[:, chunks, t, :],
+                in0=old_rows[t][:, cols].rearrange("p (c i) -> p c i", i=TC),
+                in1=pages[t % PAGES][:, cols].rearrange("p (c i) -> p c i", i=TC),
+                op=ALU.add,
+            )
+            nc.sync.dma_start(out=out_by_t[:, t, cols].rearrange("p (c i) -> p c i", i=TC), in_=y[:, chunks, t, :])
+
+        def planes(c, lo, hi, on_vector):
+            cols = slice(c * TC + lo, c * TC + hi)
+            y_bf = sb(f"y_bf{cols.start}", [P, (hi - lo) * PACK], BF16)
+            y_codes = sb(f"y_codes{cols.start}", [P, hi - lo], U32)
+            round_and_interleave(nc.vector.tensor_copy if on_vector else nc.scalar.copy, y_bf[:], y[:, c, :, lo:hi])
+            nc.vector.quantize_mx(out=y_codes[:].bitcast(FP8X4), scales=y_plane[:, cols], in_=y_bf[:])
+            nc.sync.dma_start(
+                out=out_1[0].rearrange("p c r -> p (c r)").bitcast(I32)[:, cols], in_=y_codes[:].bitcast(I32)
+            )
+
+        nc.vector.memset(gx_plane[:].bitcast(I32), 0)
+        nc.vector.memset(wvs_raw[:].bitcast(I32), 0)
+        load_plane_repeated(wgs_raw, wg_scales)
+        load_words(wg_raw, wg_words)
+        nc.sync.dma_start(out=gx_codes[:].bitcast(I32), in_=gx_words[0].rearrange("p c r -> p (c r)").bitcast(I32))
+        load_words(wv_raw, wv_words)
+        load_x(0, 0)
+        load_plane(nc.sync, gx_plane, gx_scales)
+        load_x(1, 0)
+        load_old(0)
+        load_plane(nc.sync, wvs_raw, wv_scales)
+        nc.sync.dma_start(offsets[:], offs)
+        load_old(1)
+        load_x(0, 1)
+        load_x(1, 1)
+        load_old(2)
+        load_old(3)
+
+        deal(wgs_dealt[:], wgs_raw[:], 16, slice(0, 4))
+        deal(wg_dealt[:].bitcast(U16), wg_raw[:].bitcast(U16), 8, slice(0, 4))
+        deal(wv_dealt[:].bitcast(U16), wv_raw[:].bitcast(U16), 8, slice(0, 4))
+        for page in pages:
+            nc.vector.memset(page[:], 0.0)
+        for t in range(PACK):
+            gates(t)
+        quantise_x(0, 0)
+        quantise_x(1, 0)
+        deal(wvs_dealt[:], wvs_raw[:], 16, slice(0, 2))
+        new_values(0, 0)
+        new_values(1, 0)
+        for t in range(PACK):
+            for h in range(HALVES):
+                pick(t, h)
+
+        def unit(t, h):
+            distance(t, h)
+            if (t, h) not in VECTOR_SCATTERS:
+                step(t, h)
+
+        for t in (0, 1):
+            unit(t, 0)
+            put(t, 0)
+        deal(wvs_dealt[:], wvs_raw[:], 16, slice(2, 4))
+        quantise_x(0, 1)
+        quantise_x(1, 1)
+        new_values(0, 1)
+        new_values(1, 1)
+        for t in (2, 3):
+            for h in range(HALVES):
+                new_values(t, h)
+        for t, h in ((0, 1), (1, 1), (2, 0), (2, 1)):
+            unit(t, h)
+            put(t, h)
+        unit(3, 0)
+        unit(3, 1)
+        drift(0, slice(0, 2))
+        drift(0, slice(2, 4))
+        put(3, 0)
+        put(3, 1)
+        drift(1, slice(0, 2))
+        drift(1, slice(2, 4))
+        for t in (2, 3):
+            for c in range(CHUNKS):
+                drift(t, slice(c, c + 1))
+        for piece in ROUNDS:
+            planes(*piece)
+        for q in range(4):
+            nc.scalar.dma_start(
+                out=out_2[0, 4 * q : 4 * q + 4, :].bitcast(I32), in_=y_plane[32 * q : 32 * q + 4, :].bitcast(I32)
+            )

@@ -183,8 +183,8 @@ def tile_list_page_drift_pl_kernel(
                 out=out_1[0].rearrange("p c r -> p (c r)").bitcast(I32)[:, cols], in_=y_codes[:].bitcast(I32)
             )
 
-        nc.vector.memset(gx_plane[:].bitcast(I32), 0)
-        nc.vector.memset(wvs_raw[:].bitcast(I32), 0)
+        nc.gpsimd.memset(gx_plane[:].bitcast(I32), 0)
+        nc.gpsimd.memset(wvs_raw[:].bitcast(I32), 0)
         load_plane_repeated(wgs_raw, wg_scales)
         load_words(wg_raw, wg_words)
         nc.sync.dma_start(out=gx_codes[:].bitcast(I32), in_=gx_words[0].rearrange("p c r -> p (c r)").bitcast(I32))
@@ -205,12 +205,12 @@ def tile_list_page_drift_pl_kernel(
         deal(wg_dealt[:].bitcast(U16), wg_raw[:].bitcast(U16), 8, slice(0, 4))
         deal(wv_dealt[:].bitcast(U16), wv_raw[:].bitcast(U16), 8, slice(0, 4))
         for page in pages:
-            nc.vector.memset(page[:], 0.0)
+            nc.gpsimd.memset(page[:], 0.0)
         for t in range(PACK):
             gates(t)
         quantise_x(0, 0)
         quantise_x(1, 0)
-        deal(wvs_dealt[:], wvs_raw[:], 16, slice(0, 2))
+        deal(wvs_dealt[:], wvs_raw[:], 16, slice(0, 4))
         new_values(0, 0)
         new_values(1, 0)
         for t in range(PACK):
@@ -225,7 +225,6 @@ def tile_list_page_drift_pl_kernel(
         for t in (0, 1):
             unit(t, 0)
             put(t, 0)
-        deal(wvs_dealt[:], wvs_raw[:], 16, slice(2, 4))
         quantise_x(0, 1)
         quantise_x(1, 1)
         new_values(0, 1)
@@ -233,12 +232,17 @@ def tile_list_page_drift_pl_kernel(
         for t in (2, 3):
             for h in range(HALVES):
                 new_values(t, h)
-        for t, h in ((0, 1), (1, 1), (2, 0), (2, 1)):
-            unit(t, h)
-            put(t, h)
+        for t in (0, 1):
+            unit(t, 1)
+            put(t, 1)
+        distance(2, 0)
+        distance(2, 1)
+        drift(0, slice(0, 2))
+        for h in range(HALVES):
+            step(2, h)
+            put(2, h)
         unit(3, 0)
         unit(3, 1)
-        drift(0, slice(0, 2))
         drift(0, slice(2, 4))
         put(3, 0)
         put(3, 1)

@@ -85,14 +85,6 @@ def tile_list_page_drift_pl_kernel(
                     in_=scales[:, 4 * q : 4 * q + 4, :].rearrange("z r n -> r z n").bitcast(I32),
                 )
 
-        def load_plane_repeated(tile, scales):
-            for q in range(4):
-                rows = scales[0, 4 * q : 4 * q + 4, :].bitcast(I32)
-                nc.sync.dma_start(
-                    out=tile[32 * q : 32 * q + 32, 0, :].bitcast(I32),
-                    in_=rows.unsqueeze(0).to_broadcast([8, 4, rows.shape[1]]),
-                )
-
         def load_old(t):
             nc.sync.dma_start(out=old_rows[t][:], in_=old_by_t[:, t, :])
 
@@ -148,7 +140,11 @@ def tile_list_page_drift_pl_kernel(
         steps = {th: sb(f"step{th[0]}{th[1]}", [P, JH], F32)[:] for th in picked if th not in VECTOR_SCATTERS}
 
         def pick(t, h):
-            nc.scalar.activation(out=picked[t, h], in_=old_rows[t][:].indirect(listed(h)), func=ACT.Copy)
+            columns = old_rows[t][:].indirect(listed(h))
+            if t == 0:
+                nc.vector.tensor_copy(out=picked[t, h], in_=columns)
+            else:
+                nc.scalar.activation(out=picked[t, h], in_=columns, func=ACT.Copy)
 
         def distance(t, h):
             nc.vector.tensor_tensor(out=gap[t, h], in0=v_of(t, h), in1=picked[t, h], op=ALU.subtract)
@@ -183,17 +179,15 @@ def tile_list_page_drift_pl_kernel(
                 out=out_1[0].rearrange("p c r -> p (c r)").bitcast(I32)[:, cols], in_=y_codes[:].bitcast(I32)
             )
 
-        nc.gpsimd.memset(gx_plane[:].bitcast(I32), 0)
-        nc.gpsimd.memset(wvs_raw[:].bitcast(I32), 0)
-        load_plane_repeated(wgs_raw, wg_scales)
+        for plane, scales in ((wgs_raw, wg_scales), (gx_plane, gx_scales), (wvs_raw, wv_scales)):
+            nc.vector.memset(plane[:].bitcast(I32), 0)
+            load_plane(nc.scalar, plane, scales)
         load_words(wg_raw, wg_words)
         nc.sync.dma_start(out=gx_codes[:].bitcast(I32), in_=gx_words[0].rearrange("p c r -> p (c r)").bitcast(I32))
         load_words(wv_raw, wv_words)
         load_x(0, 0)
-        load_plane(nc.sync, gx_plane, gx_scales)
         load_x(1, 0)
         load_old(0)
-        load_plane(nc.sync, wvs_raw, wv_scales)
         nc.sync.dma_start(offsets[:], offs)
         load_old(1)
         load_x(0, 1)
@@ -205,7 +199,7 @@ def tile_list_page_drift_pl_kernel(
         deal(wg_dealt[:].bitcast(U16), wg_raw[:].bitcast(U16), 8, slice(0, 4))
         deal(wv_dealt[:].bitcast(U16), wv_raw[:].bitcast(U16), 8, slice(0, 4))
         for page in pages:
-            nc.gpsimd.memset(page[:], 0.0)
+            nc.vector.memset(page[:], 0.0)
         for t in range(PACK):
             gates(t)
         quantise_x(0, 0)

@@ -24,7 +24,7 @@ JH = J // HALVES
 CHUNKS = 4
 TC = T // CHUNKS
 PAGES = 3
-VECTOR_SCATTERS = ((0, 0), (1, 1))
+VECTOR_SCATTERS = ((0, 0), (1, 1), (3, 0))
 ROUNDS = ((0, 0, TC, False), (1, 0, TC, False), (2, 0, TC // 2, False), (2, TC // 2, TC, True), (3, 0, TC, True))
 
 

from contextlib import ExitStack

import concourse.mybir as mybir

K, L, T, J, N = 1024, 512, 2048, 512, 512
FLOPS = 2 * (K + L) * N * J

F32 = mybir.dt.float32
BF16 = mybir.dt.bfloat16
I32 = mybir.dt.int32
U32 = mybir.dt.uint32
U16 = mybir.dt.uint16
U8 = mybir.dt.uint8
FP8X4 = mybir.dt.float8_e4m3fn_x4
FP4X4 = mybir.dt.float4_e2m1fn_x4
ACT = mybir.ActivationFunctionType
ALU = mybir.AluOpType

P = 128
PACK = 4
PASSES = K // (P * PACK)
HALVES = 2
JH = J // HALVES
CHUNKS = 4
TC = T // CHUNKS
PAGES = 3
VECTOR_SCATTERS = ((0, 0), (1, 1), (3, 0))
ROUNDS = ((0, 0, TC, False), (1, 0, TC, False), (2, 0, TC // 2, False), (2, TC // 2, TC, True), (3, 0, TC, True))


def tile_list_page_drift_pl_kernel(
    tc, xt, wv_words, wv_scales, gx_words, gx_scales, wg_words, wg_scales, old, offs, out_0, out_1, out_2
):
    nc = tc.nc
    with ExitStack() as ctx:
        keep = ctx.enter_context(tc.tile_pool(name="keep", bufs=1))
        psum = ctx.enter_context(tc.psum_pool(name="psum", bufs=1))

        def sb(name, shape, dtype):
            return keep.tile(shape, dtype, name=name, align_bytes=64)

        offsets = keep.tile([P, J // 16], U16, name="offsets")
        x_raw = {(z, h): sb(f"x_raw{z}{h}", [P, PACK, JH], F32) for z in range(PASSES) for h in range(HALVES)}
        x_bf = {(z, h): sb(f"x_bf{z}{h}", [P, JH * PACK], BF16) for z in range(PASSES) for h in range(HALVES)}
        x_codes = [sb(f"x_codes{z}", [P, J], U32) for z in range(PASSES)]
        x_scales = [sb(f"x_scales{z}", [P, J], U8) for z in range(PASSES)]
        wv_raw = sb("wv_raw", [P, PASSES, 2 * N], U8)
        wv_dealt = sb("wv_dealt", [P, PASSES, 2 * N], U8)
        wvs_raw = sb("wvs_raw", [P, PASSES, N], U8)
        wvs_dealt = sb("wvs_dealt", [P, PASSES, N], U8)
        wg_raw = sb("wg_raw", [P, 1, 2 * N], U8)
        wg_dealt = sb("wg_dealt", [P, 1, 2 * N], U8)
        wgs_raw = sb("wgs_raw", [P, 1, N], U8)
        wgs_dealt = sb("wgs_dealt", [P, 1, N], U8)
        gx_codes = sb("gx_codes", [P, J], U32)
        gx_plane = sb("gx_plane", [P, 1, J], U8)
        old_rows = [sb(f"old_rows{t}", [P, T], F32) for t in range(PACK)]
        pages = [sb(f"page{i}", [P, T], F32) for i in range(PAGES)]
        gate = [sb(f"gate{t}", [P, J], F32) for t in range(PACK)]
        y = sb("y", [P, CHUNKS, PACK, TC], F32)
        y_plane = sb("y_plane", [P, T], U8)
        g_bank = [psum.tile([P, J], F32, name=f"g_bank{t}") for t in range(PACK)]
        v_bank = [psum.tile([P, JH], F32, name=f"v_bank{t}") for t in range(PACK)]

        def v_of(t, h):
            return v_bank[t][:] if h == 0 else g_bank[t][:, 0:JH]

        old_by_t = old.rearrange("(p t) c -> p t c", t=PACK)
        out_by_t = out_0.rearrange("(p t) c -> p t c", t=PACK)

        def half(h):
            return slice(h * JH, (h + 1) * JH)

        def load_x(z, h):
            rows = xt[z * P * PACK : (z + 1) * P * PACK, h * JH : (h + 1) * JH]
            nc.sync.dma_start(out=x_raw[z, h][:], in_=rows.rearrange("(p i) j -> p i j", i=PACK))

        def load_words(tile, words):
            nc.sync.dma_start(out=tile[:].bitcast(I32), in_=words.rearrange("z p b -> p z b").bitcast(I32))

        def load_plane(queue, tile, scales):
            for q in range(4):
                queue.dma_start(
                    out=tile[32 * q : 32 * q + 4].bitcast(I32),
                    in_=scales[:, 4 * q : 4 * q + 4, :].rearrange("z r n -> r z n").bitcast(I32),
                )

        def load_old(t):
            nc.sync.dma_start(out=old_rows[t][:], in_=old_by_t[:, t, :])

        def deal(dealt, raw, run, ts):
            nc.vector.tensor_copy(
                out=dealt.rearrange("p z (t c i) -> p z c t i", t=PACK, i=run)[:, :, :, ts, :],
                in_=raw.rearrange("p z (c i t) -> p z c t i", t=PACK, i=run)[:, :, :, ts, :],
            )

        def round_and_interleave(copy, dst, src):
            copy(
                out=dst.rearrange("p (c i t) -> p c t i", i=4, t=PACK),
                in_=src.rearrange("p t (c i) -> p c t i", i=4),
            )

        def quantise_x(z, h):
            copy = nc.scalar.copy if (z, h) == (0, 1) else nc.vector.tensor_copy
            round_and_interleave(copy, x_bf[z, h][:], x_raw[z, h][:])
            nc.vector.quantize_mx(
                out=x_codes[z][:, half(h)].bitcast(FP8X4), scales=x_scales[z][:, half(h)], in_=x_bf[z, h][:]
            )

        def new_values(t, h):
            cols = half(h)
            for z in range(PASSES):
                nc.tensor.matmul_mx(
                    out=v_of(t, h),
                    lhsT=wv_dealt[:, z, 2 * P * t : 2 * P * (t + 1)].bitcast(FP4X4),
                    lhsT_scale=wvs_dealt[:, z, P * t : P * (t + 1)],
                    rhs=x_codes[z][:, cols].bitcast(FP8X4),
                    rhs_scale=x_scales[z][:, cols],
                    start=(z == 0),
                    stop=(z == PASSES - 1),
                )

        def gates(t):
            nc.tensor.matmul_mx(
                out=g_bank[t][:],
                lhsT=wg_dealt[:, 0, 2 * P * t : 2 * P * (t + 1)].bitcast(FP4X4),
                lhsT_scale=wgs_dealt[:, 0, P * t : P * (t + 1)],
                rhs=gx_codes[:].bitcast(FP8X4),
                rhs_scale=gx_plane[:, 0, :],
                start=True,
                stop=True,
            )
            nc.scalar.activation(out=gate[t][:], in_=g_bank[t][:], func=ACT.Sigmoid)

        def listed(h):
            return offsets[:, h * (JH // 16) : (h + 1) * (JH // 16)]

        picked = {(t, h): sb(f"picked{t}{h}", [P, JH], F32)[:] for t in range(PACK) for h in range(HALVES)}
        gap = {th: sb(f"gap{th[0]}{th[1]}", [P, JH], F32)[:] for th in picked}
        steps = {th: sb(f"step{th[0]}{th[1]}", [P, JH], F32)[:] for th in picked if th not in VECTOR_SCATTERS}

        def pick(t, h):
            columns = old_rows[t][:].indirect(listed(h))
            if t == 0:
                nc.vector.tensor_copy(out=picked[t, h], in_=columns)
            else:
                nc.scalar.activation(out=picked[t, h], in_=columns, func=ACT.Copy)

        def distance(t, h):
            nc.vector.tensor_tensor(out=gap[t, h], in0=v_of(t, h), in1=picked[t, h], op=ALU.subtract)

        def step(t, h):
            nc.vector.tensor_tensor(out=steps[t, h], in0=gap[t, h], in1=gate[t][:, half(h)], op=ALU.mult)

        def put(t, h):
            places = pages[t % PAGES][:].indirect(listed(h))
            if (t, h) in VECTOR_SCATTERS:
                nc.vector.tensor_tensor(out=places, in0=gap[t, h], in1=gate[t][:, half(h)], op=ALU.mult)
            else:
                nc.scalar.activation(out=places, in_=steps[t, h], func=ACT.Copy)

        def drift(t, chunks):
            cols = slice(chunks.start * TC, chunks.stop * TC)
            nc.vector.tensor_tensor(
                out=y[:, chunks, t, :],
                in0=old_rows[t][:, cols].rearrange("p (c i) -> p c i", i=TC),
                in1=pages[t % PAGES][:, cols].rearrange("p (c i) -> p c i", i=TC),
                op=ALU.add,
            )
            nc.sync.dma_start(out=out_by_t[:, t, cols].rearrange("p (c i) -> p c i", i=TC), in_=y[:, chunks, t, :])

        def planes(c, lo, hi, on_vector):
            cols = slice(c * TC + lo, c * TC + hi)
            y_bf = sb(f"y_bf{cols.start}", [P, (hi - lo) * PACK], BF16)
            y_codes = sb(f"y_codes{cols.start}", [P, hi - lo], U32)
            round_and_interleave(nc.vector.tensor_copy if on_vector else nc.scalar.copy, y_bf[:], y[:, c, :, lo:hi])
            nc.vector.quantize_mx(out=y_codes[:].bitcast(FP8X4), scales=y_plane[:, cols], in_=y_bf[:])
            nc.sync.dma_start(
                out=out_1[0].rearrange("p c r -> p (c r)").bitcast(I32)[:, cols], in_=y_codes[:].bitcast(I32)
            )

        for plane, scales in ((wgs_raw, wg_scales), (gx_plane, gx_scales), (wvs_raw, wv_scales)):
            nc.vector.memset(plane[:].bitcast(I32), 0)
            load_plane(nc.scalar, plane, scales)
        load_words(wg_raw, wg_words)
        nc.sync.dma_start(out=gx_codes[:].bitcast(I32), in_=gx_words[0].rearrange("p c r -> p (c r)").bitcast(I32))
        load_words(wv_raw, wv_words)
        load_x(0, 0)
        load_x(1, 0)
        load_old(0)
        nc.sync.dma_start(offsets[:], offs)
        load_old(1)
        load_x(0, 1)
        load_x(1, 1)
        load_old(2)
        load_old(3)

        deal(wgs_dealt[:], wgs_raw[:], 16, slice(0, 4))
        deal(wg_dealt[:].bitcast(U16), wg_raw[:].bitcast(U16), 8, slice(0, 4))
        deal(wv_dealt[:].bitcast(U16), wv_raw[:].bitcast(U16), 8, slice(0, 4))
        for page in pages:
            nc.vector.memset(page[:], 0.0)
        for t in range(PACK):
            gates(t)
        quantise_x(0, 0)
        quantise_x(1, 0)
        deal(wvs_dealt[:], wvs_raw[:], 16, slice(0, 4))
        new_values(0, 0)
        new_values(1, 0)
        for t in range(PACK):
            for h in range(HALVES):
                pick(t, h)

        def unit(t, h):
            distance(t, h)
            if (t, h) not in VECTOR_SCATTERS:
                step(t, h)

        for t in (0, 1):
            unit(t, 0)
            put(t, 0)
        quantise_x(0, 1)
        quantise_x(1, 1)
        new_values(0, 1)
        new_values(1, 1)
        for t in (2, 3):
            for h in range(HALVES):
                new_values(t, h)
        for t in (0, 1):
            unit(t, 1)
            put(t, 1)
        distance(2, 0)
        distance(2, 1)
        drift(0, slice(0, 2))
        for h in range(HALVES):
            step(2, h)
            put(2, h)
        unit(3, 0)
        unit(3, 1)
        drift(0, slice(2, 4))
        put(3, 0)
        put(3, 1)
        drift(1, slice(0, 2))
        drift(1, slice(2, 4))
        for t in (2, 3):
            for c in range(CHUNKS):
                drift(t, slice(c, c + 1))
        for piece in ROUNDS:
            planes(*piece)
        for q in range(4):
            nc.scalar.dma_start(
                out=out_2[0, 4 * q : 4 * q + 4, :].bitcast(I32), in_=y_plane[32 * q : 32 * q + 4, :].bitcast(I32)
            )
